import numpy as np
import ml_dtypes


def mxq(x, axis, fmt="e4m3"):
    dtype, down = {"e4m3": (ml_dtypes.float8_e4m3fn, 7), "e5m2": (ml_dtypes.float8_e5m2, 14)}[fmt]
    v = np.moveaxis(np.asarray(x, np.float32).astype(ml_dtypes.bfloat16).astype(np.float64), axis, -1)
    blocks = v.reshape(v.shape[:-1] + (-1, 32))
    amax = np.abs(blocks).max(-1, keepdims=True)
    byte = np.maximum(np.where(amax > 0, np.frexp(amax)[1] - 1 + 127, 0) - down, 1)
    scale = np.exp2(byte - 127.0)
    codes = (blocks / scale).astype(np.float32).astype(dtype).astype(np.float64)
    return np.moveaxis((codes * scale).reshape(v.shape), -1, axis)


WIDE = False


def mx_kscale(k):
    if not WIDE:
        return np.ones(k)
    levels = np.array([10, -10, 5, -5, 0])
    if k % 512:
        return np.exp2(np.random.permutation(np.resize(levels, k // 32))).repeat(32)
    a = np.empty((k // 512, 16))
    for p in range(k // 512):
        a[p, :8] = np.random.permutation(np.resize(levels, 8))
        for g in range(8):
            far = levels[np.abs(levels - a[p, g]) >= 10]
            a[p, g + 8] = far[np.random.randint(len(far))]
    return np.exp2(a.ravel()).repeat(32)


def f64(x):
    return np.asarray(x).astype(np.float64)


def striped(idx):
    return np.tile(np.asarray(idx).reshape(-1, 16).T, (8, 1)).astype(np.uint16)


def unstriped(offs):
    return offs[:16].T.reshape(-1).astype(np.int64)


E2M1 = np.array([0.0, 0.5, 1.0, 1.5, 2.0, 3.0, 4.0, 6.0, -0.0, -0.5, -1.0, -1.5, -2.0, -3.0, -4.0, -6.0])


def pack_weight(w, fmt):
    k, n = w.shape
    w = f64(np.asarray(w, np.float32).astype(ml_dtypes.bfloat16)).reshape(k // 32, 32, n)
    amax = np.abs(w).max(1)
    if fmt == "e4m3":
        byte = np.frexp(amax)[1] - 1 + 127 - 7
    else:
        mant, ex = np.frexp(amax / 6.0)
        byte = np.where(mant > 0.5, ex, ex - 1) + 127
    byte = np.clip(np.where(amax > 0, byte, 1), 1, 254)
    scaled = (w * np.exp2(127.0 - byte)[:, None, :]).reshape(k, n).astype(np.float32)
    by_word = np.ascontiguousarray(scaled.reshape(k // 512, 128, 4, n).transpose(0, 1, 3, 2))
    if fmt == "e4m3":
        words = by_word.astype(ml_dtypes.float8_e4m3fn).view(np.uint8)
    else:
        c = by_word.astype(ml_dtypes.float4_e2m1fn).view(np.uint8) & 0xF
        words = (c[..., 0::2] | (c[..., 1::2] << 4)).reshape(k // 512, 128, 2 * n)
    return np.ascontiguousarray(words), np.ascontiguousarray(byte.astype(np.uint8).reshape(k // 512, 16, n))


def unpack_weight(words, scales, fmt):
    g, _, n = scales.shape
    words = np.ascontiguousarray(words).reshape(g, 128, n, -1)
    if fmt == "e4m3":
        vals = words.view(ml_dtypes.float8_e4m3fn).astype(np.float64)
    else:
        nib = np.empty((g, 128, n, 4), np.uint8)
        nib[..., 0::2] = words & 0xF
        nib[..., 1::2] = words >> 4
        vals = E2M1[nib]
    vals = vals * np.repeat(np.exp2(scales.astype(np.float64) - 127.0), 8, axis=1)[..., None]
    return vals.transpose(0, 1, 3, 2).reshape(g * 512, n)


K, T, J, L, I, M, N = 512, 2048, 1024, 512, 512, 512, 512


def setup_inputs():
    n = np.random.standard_normal
    idx = np.random.permutation(T)[:J]
    idx2 = np.random.permutation(J)[:I]
    fk = mx_kscale(K)
    fl = mx_kscale(L)
    fm = mx_kscale(M)
    xqp = pack_weight(n((K, T)) / fk[:, None], "e2m1")
    wap = pack_weight(n((K, N)) * 1 / np.sqrt(K) * fk[:, None], "e4m3")
    xbp = pack_weight(n((L, J)) / fl[:, None], "e2m1")
    wbp = pack_weight(n((L, N)) * 1 / np.sqrt(L) * fl[:, None], "e4m3")
    wcp = pack_weight(n((M, N)) * 1 / np.sqrt(M) * fm[:, None], "e4m3")
    return {
        "xq_words": xqp[0],
        "xq_scales": xqp[1],
        "wa_words": wap[0],
        "wa_scales": wap[1],
        "xb_words": xbp[0],
        "xb_scales": xbp[1],
        "wb_words": wbp[0],
        "wb_scales": wbp[1],
        "xc": (n((M, I)) / fm[:, None]).astype(np.float32),
        "wc_words": wcp[0],
        "wc_scales": wcp[1],
        "offs": striped(idx),
        "offs2": striped(idx2),
    }


def reference(xq_words, xq_scales, wa_words, wa_scales, xb_words, xb_scales, wb_words, wb_scales, xc, wc_words, wc_scales, offs, offs2):
    idx = unstriped(offs)
    idx2 = unstriped(offs2)
    xqu = unpack_weight(xq_words, xq_scales, "e2m1")
    wau = unpack_weight(wa_words, wa_scales, "e4m3")
    xbu = unpack_weight(xb_words, xb_scales, "e2m1")
    wbu = unpack_weight(wb_words, wb_scales, "e4m3")
    wcu = unpack_weight(wc_words, wc_scales, "e4m3")
    z = wau.T @ xqu
    p = wbu.T @ xbu
    xcq = mxq(f64(xc), 0, "e4m3")
    q = wcu.T @ xcq
    qs = np.zeros((N, J))
    qs[:, idx2] = q
    s = p + qs
    sp = np.zeros((N, T))
    sp[:, idx] = s
    y = z + sp
    return y

@@ -1,0 +1,224 @@
+from contextlib import ExitStack
+
+import concourse.mybir as mybir
+from concourse.masks import make_identity
+
+K, T, J, I, N = 512, 2048, 1024, 512, 512
+FLOPS = 2 * K * N * (T + J + I)
+
+F32 = mybir.dt.float32
+BF16 = mybir.dt.bfloat16
+I32 = mybir.dt.int32
+U32 = mybir.dt.uint32
+U16 = mybir.dt.uint16
+U8 = mybir.dt.uint8
+FP8X4 = mybir.dt.float8_e4m3fn_x4
+FP4X4 = mybir.dt.float4_e2m1fn_x4
+ADD = mybir.AluOpType.add
+
+P = 128
+PACK = 4
+BANK = 512
+BANKS = 8
+ROW_TILES = N // P
+CHUNKS = ((0, 128), (128, 256), (256, 512))
+FILL = 512
+
+
+def tile_list_three_tiers_nested_kernel(tc, xq_words, xq_scales, wa_words, wa_scales, xb_words, xb_scales, wb_words, wb_scales, xc, wc_words, wc_scales, offs, offs2, out):
+    nc = tc.nc
+    with ExitStack() as ctx:
+        keep = ctx.enter_context(tc.tile_pool(name="keep", bufs=1))
+        ring = ctx.enter_context(tc.tile_pool(name="ring", bufs=8))
+        psum = ctx.enter_context(tc.psum_pool(name="psum", bufs=1))
+
+        idx = keep.tile([P, J // 16], U16, name="idx")
+        idx2 = keep.tile([P, I // 16], U16, name="idx2")
+
+        def held(name, shape, dtype):
+            return keep.tile(shape, dtype, name=name, align_bytes=64)
+
+        wa = held("wa", [P, N], U32)
+        wb = held("wb", [P, N], U32)
+        wc = held("wc", [P, N], U32)
+        xq = held("xq", [P, 2 * T], U8)
+        xb = held("xb", [P, 2 * J], U8)
+        wc_s = held("wc_s", [P, N], U8)
+        second_s = held("second_s", [P, N + J], U8)
+        base_s = held("base_s", [P, N + T], U8)
+        wb_s, xb_s = second_s[:, 0:N], second_s[:, N : N + J]
+        wa_s, xq_s = base_s[:, 0:N], base_s[:, N : N + T]
+        xc_raw = [held("xc_raw%d" % c, [P, PACK, hi - lo], F32) for c, (lo, hi) in enumerate(CHUNKS)]
+        xc_bf = [held("xc_bf%d" % c, [P, hi - lo, PACK], BF16) for c, (lo, hi) in enumerate(CHUNKS)]
+        xcq = held("xcq", [P, I], U32)
+        xcq_s = held("xcq_s", [P, I], U8)
+        q_sb = [held("q_sb%d" % r, [P, I], F32) for r in range(ROW_TILES)]
+        p_sb = [held("p_sb%d" % r, [P, J], F32) for r in range(ROW_TILES)]
+        z_sb = [held("z_sb%d" % r, [P, T], F32) for r in range(ROW_TILES - 1)]
+        qs = [held("qs%d" % b, [P, J], F32) for b in range(2)]
+        sp = [held("sp%d" % b, [P, T], F32) for b in range(2)]
+        ident = held("ident", [P, P], F32)
+        banks = [psum.tile([P, BANK], F32, name="bank%d" % b) for b in range(BANKS)]
+        free = list(range(BANKS))
+
+        def next_bank(keep_it=False):
+            b = free[0]
+            free.remove(b)
+            if not keep_it:
+                free.append(b)
+            return banks[b]
+
+        def load_words(dst, src):
+            nc.sync.dma_start(out=dst[:].bitcast(I32), in_=src.bitcast(I32))
+
+        def load_fp8(dst, words):
+            load_words(dst, words[0].rearrange("p n t -> p (n t)"))
+
+        def load_scales(dst, scales):
+            for quad in range(4):
+                nc.sync.dma_start(out=dst[32 * quad : 32 * quad + 4, :].bitcast(I32), in_=scales[0, 4 * quad : 4 * quad + 4, :].bitcast(I32))
+
+        def load_xc(c):
+            lo, hi = CHUNKS[c]
+            nc.sync.dma_start(out=xc_raw[c][:], in_=xc[:, lo:hi].rearrange("(p t) w -> p t w", t=PACK))
+
+        nc.vector.memset(wc_s[:].bitcast(I32), 0)
+        nc.vector.memset(second_s[:].bitcast(I32), 0)
+        nc.vector.memset(base_s[:].bitcast(I32), 0)
+
+        load_xc(0)
+        load_scales(wc_s[:], wc_scales)
+        load_fp8(wc, wc_words)
+        nc.sync.dma_start(idx2[:], offs2)
+        load_xc(1)
+        load_xc(2)
+        load_fp8(wb, wb_words)
+        load_words(xb, xb_words[0])
+        load_scales(wb_s, wb_scales)
+        load_scales(xb_s, xb_scales)
+        nc.sync.dma_start(idx[:], offs)
+        load_fp8(wa, wa_words)
+        load_words(xq, xq_words[0])
+        load_scales(wa_s, wa_scales)
+        load_scales(xq_s, xq_scales)
+        make_identity(nc, ident[:])
+
+        def weave(c, copy):
+            copy(out=xc_bf[c][:].rearrange("p (g i) t -> p g t i", i=4), in_=xc_raw[c][:].rearrange("p t (g i) -> p g t i", i=4))
+
+        def quantize(c):
+            lo, hi = CHUNKS[c]
+            nc.vector.quantize_mx(out=xcq[:, lo:hi].bitcast(FP8X4), scales=xcq_s[:, lo:hi], in_=xc_bf[c][:].rearrange("p w t -> p (w t)"))
+
+        def product(bank, w, w_s, r, x, x_s):
+            rows = slice(r * P, (r + 1) * P)
+            nc.tensor.matmul_mx(out=bank, lhsT=w[:, rows].bitcast(FP8X4), lhsT_scale=w_s[:, rows], rhs=x, rhs_scale=x_s, start=True, stop=True)
+
+        def third(r, lo, hi, dst):
+            bank = next_bank()[:, 0 : hi - lo]
+            product(bank, wc, wc_s, r, xcq[:, lo:hi].bitcast(FP8X4), xcq_s[:, lo:hi])
+            nc.scalar.copy(out=dst, in_=bank)
+
+        def fp4_product(bank, w, w_s, r, x, x_s, g):
+            product(bank[:], w, w_s, r, x[:, 2 * BANK * g : 2 * BANK * (g + 1)].bitcast(FP4X4), x_s[:, BANK * g : BANK * (g + 1)])
+
+        def second(r, g):
+            bank = next_bank()
+            fp4_product(bank, wb, wb_s, r, xb, xb_s, g)
+            nc.scalar.copy(out=p_sb[r][:, BANK * g : BANK * (g + 1)], in_=bank[:])
+
+        def base(r, g):
+            bank = next_bank()
+            fp4_product(bank, wa, wa_s, r, xq, xq_s, g)
+            nc.scalar.copy(out=z_sb[r][:, BANK * g : BANK * (g + 1)], in_=bank[:])
+
+        def place_q(window, src, lo, hi):
+            nc.vector.tensor_copy(window[:].indirect(idx2[:, lo // 16 : hi // 16]), src)
+
+        def place_s(r, q_window):
+            nc.vector.tensor_tensor(sp[r % 2][:].indirect(idx[:]), p_sb[r][:], q_window[:], ADD)
+
+        def clear(window):
+            for lo in range(0, window.shape[1], FILL):
+                nc.vector.memset(window[:, lo : lo + FILL], 0.0)
+
+        def add_turned(r, g):
+            bank = next_bank()
+            for j in range(BANK // P):
+                cols = slice(BANK * g + P * j, BANK * g + P * (j + 1))
+                dst = bank[:, P * j : P * (j + 1)]
+                nc.tensor.matmul(dst, z_sb[r][:, cols], ident[:], start=True, stop=False, is_transpose=True)
+                nc.tensor.matmul(dst, sp[r % 2][:, cols], ident[:], start=False, stop=True, is_transpose=True)
+            turned = ring.tile([P, BANK], F32, name="turned")
+            nc.scalar.copy(out=turned[:], in_=bank[:])
+            return turned
+
+        def turn_back(r, g, turned):
+            bank = next_bank()
+            for j in range(BANK // P):
+                nc.tensor.transpose(bank[:, P * j : P * (j + 1)], turned[:, P * j : P * (j + 1)], ident[:])
+            result = ring.tile([P, BANK], F32, name="result")
+            nc.scalar.copy(out=result[:], in_=bank[:])
+            nc.sync.dma_start(out=out[r * P : (r + 1) * P, BANK * g : BANK * (g + 1)], in_=result[:])
+
+        def finish(r, fillers):
+            turned = [add_turned(r, 0)]
+            for g in range(T // BANK):
+                fillers[g]()
+                if g + 1 < T // BANK:
+                    turned.append(add_turned(r, g + 1))
+                turn_back(r, g, turned[g])
+
+        weave(0, nc.vector.tensor_copy)
+        quantize(0)
+        weave(1, nc.scalar.copy)
+        quantize(1)
+        clear(qs[0])
+        clear(qs[1])
+        for c in range(2):
+            lo, hi = CHUNKS[c]
+            if c == 1:
+                weave(2, nc.scalar.copy)
+                quantize(2)
+            for r in range(2):
+                dst = xc_raw[2][:, 0, 0 : hi - lo] if (c, r) == (1, 1) else q_sb[r][:, lo:hi]
+                third(r, lo, hi, dst)
+                place_q(qs[r], dst, lo, hi)
+        lo, hi = CHUNKS[2]
+        for r in range(2):
+            third(r, lo, hi, q_sb[r][:, lo:hi])
+            place_q(qs[r], q_sb[r][:, lo:hi], lo, hi)
+        clear(sp[0])
+        clear(sp[1])
+
+        for r in range(2):
+            for g in range(J // BANK):
+                second(r, g)
+        for r in range(2, ROW_TILES):
+            third(r, 0, I, q_sb[r][:])
+        for r in range(2):
+            for g in range(T // BANK):
+                base(r, g)
+
+        place_s(0, qs[0])
+        place_s(1, qs[1])
+        finish(0, [lambda: second(2, 0), lambda: second(2, 1), lambda: base(2, 0), lambda: base(2, 1)])
+        place_q(qs[0], q_sb[2][:], 0, I)
+        place_s(2, qs[0])
+        finish(1, [lambda: base(2, 2), lambda: base(2, 3), lambda: second(3, 0), lambda: second(3, 1)])
+        place_q(qs[0], q_sb[3][:], 0, I)
+        place_s(3, qs[0])
+
+        last = ROW_TILES - 1
+        z_last = []
+
+        def base_last():
+            bank = next_bank(True)
+            fp4_product(bank, wa, wa_s, last, xq, xq_s, len(z_last))
+            z_last.append(bank)
+
+        finish(2, [base_last] * (T // BANK))
+        for g in range(T // BANK):
+            result = ring.tile([P, BANK], F32, name="result")
+            nc.vector.tensor_tensor(result[:], z_last[g][:], sp[last % 2][:, BANK * g : BANK * (g + 1)], ADD)
+            nc.sync.dma_start(out=out[last * P : (last + 1) * P, BANK * g : BANK * (g + 1)], in_=result[:])

@@ -23,6 +23,7 @@ BANKS = 8
 ROW_TILES = N // P
 CHUNKS = ((0, 128), (128, 256), (256, 512))
 FILL = 512
+GP_COLS = 1280
 
 
 def tile_list_three_tiers_nested_kernel(tc, xq_words, xq_scales, wa_words, wa_scales, xb_words, xb_scales, wb_words, wb_scales, xc, wc_words, wc_scales, offs, offs2, out):
@@ -35,8 +36,8 @@ def tile_list_three_tiers_nested_kernel(tc, xq_words, xq_scales, wa_words, wa_sc
         idx = keep.tile([P, J // 16], U16, name="idx")
         idx2 = keep.tile([P, I // 16], U16, name="idx2")
 
-        def held(name, shape, dtype):
-            return keep.tile(shape, dtype, name=name, align_bytes=64)
+        def held(name, shape, dtype, tag=None):
+            return keep.tile(shape, dtype, name=name, tag=tag or name, align_bytes=64)
 
         wa = held("wa", [P, N], U32)
         wb = held("wb", [P, N], U32)
@@ -50,22 +51,23 @@ def tile_list_three_tiers_nested_kernel(tc, xq_words, xq_scales, wa_words, wa_sc
         wa_s, xq_s = base_s[:, 0:N], base_s[:, N : N + T]
         xc_raw = [held("xc_raw%d" % c, [P, PACK, hi - lo], F32) for c, (lo, hi) in enumerate(CHUNKS)]
         xc_bf = [held("xc_bf%d" % c, [P, hi - lo, PACK], BF16) for c, (lo, hi) in enumerate(CHUNKS)]
+        gp_sum = [held("gp_sum%d" % b, [P, GP_COLS], F32) for b in range(2)]
         xcq = held("xcq", [P, I], U32)
         xcq_s = held("xcq_s", [P, I], U8)
         q_sb = [held("q_sb%d" % r, [P, I], F32) for r in range(ROW_TILES)]
         p_sb = [held("p_sb%d" % r, [P, J], F32) for r in range(ROW_TILES)]
         z_sb = [held("z_sb%d" % r, [P, T], F32) for r in range(ROW_TILES - 1)]
         qs = [held("qs%d" % b, [P, J], F32) for b in range(2)]
-        sp = [held("sp%d" % b, [P, T], F32) for b in range(2)]
+        q_late = held("q_late", [P, CHUNKS[2][1] - CHUNKS[2][0]], F32)
+        sp = []
         ident = held("ident", [P, P], F32)
         banks = [psum.tile([P, BANK], F32, name="bank%d" % b) for b in range(BANKS)]
         free = list(range(BANKS))
 
-        def next_bank(keep_it=False):
+        def next_bank():
             b = free[0]
             free.remove(b)
-            if not keep_it:
-                free.append(b)
+            free.append(b)
             return banks[b]
 
         def load_words(dst, src):
@@ -127,47 +129,56 @@ def tile_list_three_tiers_nested_kernel(tc, xq_words, xq_scales, wa_words, wa_sc
             fp4_product(bank, wb, wb_s, r, xb, xb_s, g)
             nc.scalar.copy(out=p_sb[r][:, BANK * g : BANK * (g + 1)], in_=bank[:])
 
-        def base(r, g):
-            bank = next_bank()
+        def base(r, g, bank):
             fp4_product(bank, wa, wa_s, r, xq, xq_s, g)
-            nc.scalar.copy(out=z_sb[r][:, BANK * g : BANK * (g + 1)], in_=bank[:])
+            if r < ROW_TILES - 1:
+                nc.scalar.copy(out=z_sb[r][:, BANK * g : BANK * (g + 1)], in_=bank[:])
 
         def place_q(window, src, lo, hi):
             nc.vector.tensor_copy(window[:].indirect(idx2[:, lo // 16 : hi // 16]), src)
 
         def place_s(r, q_window):
-            nc.vector.tensor_tensor(sp[r % 2][:].indirect(idx[:]), p_sb[r][:], q_window[:], ADD)
+            nc.vector.tensor_tensor(sp[r % 3][:].indirect(idx[:]), p_sb[r][:], q_window[:], ADD)
 
         def clear(window):
             for lo in range(0, window.shape[1], FILL):
                 nc.vector.memset(window[:, lo : lo + FILL], 0.0)
 
-        def add_turned(r, g):
+        def add_turned(r, lo, hi):
             bank = next_bank()
-            for j in range(BANK // P):
-                cols = slice(BANK * g + P * j, BANK * g + P * (j + 1))
-                dst = bank[:, P * j : P * (j + 1)]
-                nc.tensor.matmul(dst, z_sb[r][:, cols], ident[:], start=True, stop=False, is_transpose=True)
-                nc.tensor.matmul(dst, sp[r % 2][:, cols], ident[:], start=False, stop=True, is_transpose=True)
+            for c in range(lo, hi, P):
+                dst = bank[:, c - lo : c - lo + P]
+                nc.tensor.matmul(dst, z_sb[r][:, c : c + P], ident[:], start=True, stop=False, is_transpose=True)
+                nc.tensor.matmul(dst, sp[r % 3][:, c : c + P], ident[:], start=False, stop=True, is_transpose=True)
             turned = ring.tile([P, BANK], F32, name="turned")
-            nc.scalar.copy(out=turned[:], in_=bank[:])
+            nc.scalar.copy(out=turned[:, 0 : hi - lo], in_=bank[:, 0 : hi - lo])
             return turned
 
-        def turn_back(r, g, turned):
+        def turn_back(r, lo, hi, turned):
             bank = next_bank()
-            for j in range(BANK // P):
-                nc.tensor.transpose(bank[:, P * j : P * (j + 1)], turned[:, P * j : P * (j + 1)], ident[:])
+            for c in range(0, hi - lo, P):
+                nc.tensor.transpose(bank[:, c : c + P], turned[:, c : c + P], ident[:])
             result = ring.tile([P, BANK], F32, name="result")
-            nc.scalar.copy(out=result[:], in_=bank[:])
-            nc.sync.dma_start(out=out[r * P : (r + 1) * P, BANK * g : BANK * (g + 1)], in_=result[:])
+            nc.scalar.copy(out=result[:, 0 : hi - lo], in_=bank[:, 0 : hi - lo])
+            nc.scalar.dma_start(out=out[r * P : (r + 1) * P, lo:hi], in_=result[:, 0 : hi - lo])
 
-        def finish(r, fillers):
-            turned = [add_turned(r, 0)]
-            for g in range(T // BANK):
-                fillers[g]()
-                if g + 1 < T // BANK:
-                    turned.append(add_turned(r, g + 1))
-                turn_back(r, g, turned[g])
+        def finish_turned(r, first):
+            spans = [(lo, min(lo + BANK, T)) for lo in range(first, T, BANK)]
+            turned = [add_turned(r, *spans[0])]
+            for g, (lo, hi) in enumerate(spans):
+                if g + 1 < len(spans):
+                    turned.append(add_turned(r, *spans[g + 1]))
+                turn_back(r, lo, hi, turned[g])
+
+        def finish_gpsimd(r):
+            result = gp_sum[r - 1]
+            nc.gpsimd.tensor_tensor(result[:], z_sb[r][:, 0:GP_COLS], sp[r % 3][:, 0:GP_COLS], ADD)
+            nc.sync.dma_start(out=out[r * P : (r + 1) * P, 0:GP_COLS], in_=result[:])
+
+        def finish_vector(r, g, bank):
+            cols = slice(BANK * g, BANK * (g + 1))
+            nc.vector.tensor_tensor(z_sb[r - 1][:, cols], bank[:], sp[r % 3][:, cols], ADD)
+            nc.sync.dma_start(out=out[r * P : (r + 1) * P, cols], in_=z_sb[r - 1][:, cols])
 
         weave(0, nc.vector.tensor_copy)
         quantize(0)
@@ -186,39 +197,36 @@ def tile_list_three_tiers_nested_kernel(tc, xq_words, xq_scales, wa_words, wa_sc
                 place_q(qs[r], dst, lo, hi)
         lo, hi = CHUNKS[2]
         for r in range(2):
-            third(r, lo, hi, q_sb[r][:, lo:hi])
-            place_q(qs[r], q_sb[r][:, lo:hi], lo, hi)
-        clear(sp[0])
-        clear(sp[1])
+            dst = q_late[:] if r == 1 else q_sb[r][:, lo:hi]
+            third(r, lo, hi, dst)
+            place_q(qs[r], dst, lo, hi)
+        for b, tag in enumerate(("xc_bf2", "xc_raw2", "q_late")):
+            sp.append(held("sp%d" % b, [P, T], F32, tag))
+            nc.gpsimd.memset(sp[b][:], 0.0)
 
-        for r in range(2):
-            for g in range(J // BANK):
-                second(r, g)
+        groups = T // BANK
         for r in range(2, ROW_TILES):
             third(r, 0, I, q_sb[r][:])
-        for r in range(2):
-            for g in range(T // BANK):
-                base(r, g)
+        for r in range(ROW_TILES):
+            for g in range(J // BANK):
+                second(r, g)
+        for g in range(groups):
+            base(0, g, next_bank())
+        z_banks = [banks[b] for b in free[:groups]]
+        for b in free[:groups]:
+            free.remove(b)
+        for g in range(groups):
+            base(1, g, z_banks[g])
 
         place_s(0, qs[0])
         place_s(1, qs[1])
-        finish(0, [lambda: second(2, 0), lambda: second(2, 1), lambda: base(2, 0), lambda: base(2, 1)])
-        place_q(qs[0], q_sb[2][:], 0, I)
-        place_s(2, qs[0])
-        finish(1, [lambda: base(2, 2), lambda: base(2, 3), lambda: second(3, 0), lambda: second(3, 1)])
-        place_q(qs[0], q_sb[3][:], 0, I)
-        place_s(3, qs[0])
-
-        last = ROW_TILES - 1
-        z_last = []
-
-        def base_last():
-            bank = next_bank(True)
-            fp4_product(bank, wa, wa_s, last, xq, xq_s, len(z_last))
-            z_last.append(bank)
-
-        finish(2, [base_last] * (T // BANK))
-        for g in range(T // BANK):
-            result = ring.tile([P, BANK], F32, name="result")
-            nc.vector.tensor_tensor(result[:], z_last[g][:], sp[last % 2][:, BANK * g : BANK * (g + 1)], ADD)
-            nc.sync.dma_start(out=out[last * P : (last + 1) * P, BANK * g : BANK * (g + 1)], in_=result[:])
+        finish_turned(0, 0)
+        for r in range(1, ROW_TILES - 1):
+            finish_gpsimd(r)
+            place_q(qs[1], q_sb[r + 1][:], 0, I)
+            place_s(r + 1, qs[1])
+            for g in range(groups):
+                base(r + 1, g, z_banks[g])
+            finish_turned(r, GP_COLS)
+        for g in range(groups):
+            finish_vector(ROW_TILES - 1, g, z_banks[g])

@@ -1,7 +1,6 @@
 from contextlib import ExitStack
 
 import concourse.mybir as mybir
-from concourse.masks import make_identity
 
 K, T, J, I, N = 512, 2048, 1024, 512, 512
 FLOPS = 2 * K * N * (T + J + I)
@@ -23,14 +22,14 @@ BANKS = 8
 ROW_TILES = N // P
 CHUNKS = ((0, 128), (128, 256), (256, 512))
 FILL = 512
-GP_COLS = 1280
+HALF = T // 2
+TAIL = ((0, 256), (256, 512), (512, 1024), (1024, 1536))
 
 
 def tile_list_three_tiers_nested_kernel(tc, xq_words, xq_scales, wa_words, wa_scales, xb_words, xb_scales, wb_words, wb_scales, xc, wc_words, wc_scales, offs, offs2, out):
     nc = tc.nc
     with ExitStack() as ctx:
         keep = ctx.enter_context(tc.tile_pool(name="keep", bufs=1))
-        ring = ctx.enter_context(tc.tile_pool(name="ring", bufs=8))
         psum = ctx.enter_context(tc.psum_pool(name="psum", bufs=1))
 
         idx = keep.tile([P, J // 16], U16, name="idx")
@@ -41,7 +40,7 @@ def tile_list_three_tiers_nested_kernel(tc, xq_words, xq_scales, wa_words, wa_sc
 
         wa = held("wa", [P, N], U32)
         wb = held("wb", [P, N], U32)
-        wc = held("wc", [P, N], U32)
+        wc = [held("wc%d" % h, [P, N // 2], U32) for h in range(2)]
         xq = held("xq", [P, 2 * T], U8)
         xb = held("xb", [P, 2 * J], U8)
         wc_s = held("wc_s", [P, N], U8)
@@ -51,16 +50,15 @@ def tile_list_three_tiers_nested_kernel(tc, xq_words, xq_scales, wa_words, wa_sc
         wa_s, xq_s = base_s[:, 0:N], base_s[:, N : N + T]
         xc_raw = [held("xc_raw%d" % c, [P, PACK, hi - lo], F32) for c, (lo, hi) in enumerate(CHUNKS)]
         xc_bf = [held("xc_bf%d" % c, [P, hi - lo, PACK], BF16) for c, (lo, hi) in enumerate(CHUNKS)]
-        gp_sum = [held("gp_sum%d" % b, [P, GP_COLS], F32) for b in range(2)]
         xcq = held("xcq", [P, I], U32)
         xcq_s = held("xcq_s", [P, I], U8)
         q_sb = [held("q_sb%d" % r, [P, I], F32) for r in range(ROW_TILES)]
         p_sb = [held("p_sb%d" % r, [P, J], F32) for r in range(ROW_TILES)]
+        s_sb = [held("s_sb%d" % r, [P, J], F32) for r in range(ROW_TILES)]
         z_sb = [held("z_sb%d" % r, [P, T], F32) for r in range(ROW_TILES - 1)]
+        y_sb = [held("y_sb%d" % r, [P, T], F32) for r in range(ROW_TILES - 1)]
+        z_end = held("z_end", [P, BANK], F32)
         qs = [held("qs%d" % b, [P, J], F32) for b in range(2)]
-        q_late = held("q_late", [P, CHUNKS[2][1] - CHUNKS[2][0]], F32)
-        sp = []
-        ident = held("ident", [P, P], F32)
         banks = [psum.tile([P, BANK], F32, name="bank%d" % b) for b in range(BANKS)]
         free = list(range(BANKS))
 
@@ -90,10 +88,12 @@ def tile_list_three_tiers_nested_kernel(tc, xq_words, xq_scales, wa_words, wa_sc
 
         load_xc(0)
         load_scales(wc_s[:], wc_scales)
-        load_fp8(wc, wc_words)
+        wc_rows = wc_words[0].rearrange("p n t -> p (n t)")
+        load_words(wc[0], wc_rows[:, 0 : 2 * N])
         nc.sync.dma_start(idx2[:], offs2)
         load_xc(1)
         load_xc(2)
+        load_words(wc[1], wc_rows[:, 2 * N : 4 * N])
         load_fp8(wb, wb_words)
         load_words(xb, xb_words[0])
         load_scales(wb_s, wb_scales)
@@ -103,7 +103,6 @@ def tile_list_three_tiers_nested_kernel(tc, xq_words, xq_scales, wa_words, wa_sc
         load_words(xq, xq_words[0])
         load_scales(wa_s, wa_scales)
         load_scales(xq_s, xq_scales)
-        make_identity(nc, ident[:])
 
         def weave(c, copy):
             copy(out=xc_bf[c][:].rearrange("p (g i) t -> p g t i", i=4), in_=xc_raw[c][:].rearrange("p t (g i) -> p g t i", i=4))
@@ -113,72 +112,40 @@ def tile_list_three_tiers_nested_kernel(tc, xq_words, xq_scales, wa_words, wa_sc
             nc.vector.quantize_mx(out=xcq[:, lo:hi].bitcast(FP8X4), scales=xcq_s[:, lo:hi], in_=xc_bf[c][:].rearrange("p w t -> p (w t)"))
 
         def product(bank, w, w_s, r, x, x_s):
-            rows = slice(r * P, (r + 1) * P)
-            nc.tensor.matmul_mx(out=bank, lhsT=w[:, rows].bitcast(FP8X4), lhsT_scale=w_s[:, rows], rhs=x, rhs_scale=x_s, start=True, stop=True)
+            nc.tensor.matmul_mx(out=bank, lhsT=w.bitcast(FP8X4), lhsT_scale=w_s[:, r * P : (r + 1) * P], rhs=x, rhs_scale=x_s, start=True, stop=True)
 
         def third(r, lo, hi, dst):
             bank = next_bank()[:, 0 : hi - lo]
-            product(bank, wc, wc_s, r, xcq[:, lo:hi].bitcast(FP8X4), xcq_s[:, lo:hi])
+            product(bank, wc[r // 2][:, r % 2 * P : (r % 2 + 1) * P], wc_s, r, xcq[:, lo:hi].bitcast(FP8X4), xcq_s[:, lo:hi])
             nc.scalar.copy(out=dst, in_=bank)
 
         def fp4_product(bank, w, w_s, r, x, x_s, g):
-            product(bank[:], w, w_s, r, x[:, 2 * BANK * g : 2 * BANK * (g + 1)].bitcast(FP4X4), x_s[:, BANK * g : BANK * (g + 1)])
+            product(bank[:], w[:, r * P : (r + 1) * P], w_s, r, x[:, 2 * BANK * g : 2 * BANK * (g + 1)].bitcast(FP4X4), x_s[:, BANK * g : BANK * (g + 1)])
 
         def second(r, g):
             bank = next_bank()
             fp4_product(bank, wb, wb_s, r, xb, xb_s, g)
             nc.scalar.copy(out=p_sb[r][:, BANK * g : BANK * (g + 1)], in_=bank[:])
 
-        def base(r, g, bank):
+        def base(r, g, dst):
+            bank = next_bank()
             fp4_product(bank, wa, wa_s, r, xq, xq_s, g)
-            if r < ROW_TILES - 1:
-                nc.scalar.copy(out=z_sb[r][:, BANK * g : BANK * (g + 1)], in_=bank[:])
+            if dst is not None:
+                nc.scalar.copy(out=dst, in_=bank[:])
+            return bank
 
         def place_q(window, src, lo, hi):
             nc.vector.tensor_copy(window[:].indirect(idx2[:, lo // 16 : hi // 16]), src)
 
-        def place_s(r, q_window):
-            nc.vector.tensor_tensor(sp[r % 3][:].indirect(idx[:]), p_sb[r][:], q_window[:], ADD)
+        def place_s(r):
+            nc.vector.tensor_copy(sp[r % 2][:].indirect(idx[:]), s_sb[r][:])
+
+        def store(r, lo, hi, src):
+            nc.sync.dma_start(out=out[r * P : (r + 1) * P, lo:hi], in_=src[:, lo:hi])
 
         def clear(window):
             for lo in range(0, window.shape[1], FILL):
                 nc.vector.memset(window[:, lo : lo + FILL], 0.0)
-
-        def add_turned(r, lo, hi):
-            bank = next_bank()
-            for c in range(lo, hi, P):
-                dst = bank[:, c - lo : c - lo + P]
-                nc.tensor.matmul(dst, z_sb[r][:, c : c + P], ident[:], start=True, stop=False, is_transpose=True)
-                nc.tensor.matmul(dst, sp[r % 3][:, c : c + P], ident[:], start=False, stop=True, is_transpose=True)
-            turned = ring.tile([P, BANK], F32, name="turned")
-            nc.scalar.copy(out=turned[:, 0 : hi - lo], in_=bank[:, 0 : hi - lo])
-            return turned
-
-        def turn_back(r, lo, hi, turned):
-            bank = next_bank()
-            for c in range(0, hi - lo, P):
-                nc.tensor.transpose(bank[:, c : c + P], turned[:, c : c + P], ident[:])
-            result = ring.tile([P, BANK], F32, name="result")
-            nc.scalar.copy(out=result[:, 0 : hi - lo], in_=bank[:, 0 : hi - lo])
-            nc.scalar.dma_start(out=out[r * P : (r + 1) * P, lo:hi], in_=result[:, 0 : hi - lo])
-
-        def finish_turned(r, first):
-            spans = [(lo, min(lo + BANK, T)) for lo in range(first, T, BANK)]
-            turned = [add_turned(r, *spans[0])]
-            for g, (lo, hi) in enumerate(spans):
-                if g + 1 < len(spans):
-                    turned.append(add_turned(r, *spans[g + 1]))
-                turn_back(r, lo, hi, turned[g])
-
-        def finish_gpsimd(r):
-            result = gp_sum[r - 1]
-            nc.gpsimd.tensor_tensor(result[:], z_sb[r][:, 0:GP_COLS], sp[r % 3][:, 0:GP_COLS], ADD)
-            nc.sync.dma_start(out=out[r * P : (r + 1) * P, 0:GP_COLS], in_=result[:])
-
-        def finish_vector(r, g, bank):
-            cols = slice(BANK * g, BANK * (g + 1))
-            nc.vector.tensor_tensor(z_sb[r - 1][:, cols], bank[:], sp[r % 3][:, cols], ADD)
-            nc.sync.dma_start(out=out[r * P : (r + 1) * P, cols], in_=z_sb[r - 1][:, cols])
 
         weave(0, nc.vector.tensor_copy)
         quantize(0)
@@ -197,36 +164,39 @@ def tile_list_three_tiers_nested_kernel(tc, xq_words, xq_scales, wa_words, wa_sc
                 place_q(qs[r], dst, lo, hi)
         lo, hi = CHUNKS[2]
         for r in range(2):
-            dst = q_late[:] if r == 1 else q_sb[r][:, lo:hi]
-            third(r, lo, hi, dst)
-            place_q(qs[r], dst, lo, hi)
-        for b, tag in enumerate(("xc_bf2", "xc_raw2", "q_late")):
-            sp.append(held("sp%d" % b, [P, T], F32, tag))
-            nc.gpsimd.memset(sp[b][:], 0.0)
-
-        groups = T // BANK
+            third(r, lo, hi, q_sb[r][:, lo:hi])
+            place_q(qs[r], q_sb[r][:, lo:hi], lo, hi)
         for r in range(2, ROW_TILES):
             third(r, 0, I, q_sb[r][:])
+        for r, tag in ((2, "xc_bf2"), (3, "xc_raw2")):
+            qs.append(held("qs%d" % r, [P, J], F32, tag))
+            nc.gpsimd.memset(qs[r][:], 0.0)
+            place_q(qs[r], q_sb[r][:], 0, I)
+        sp = [held("sp0", [P, T], F32, "wc1"), held("sp1", [P, T], F32, "xcq")]
+        for window in sp:
+            nc.gpsimd.memset(window[:], 0.0)
+
+        groups = T // BANK
+        last = ROW_TILES - 1
         for r in range(ROW_TILES):
             for g in range(J // BANK):
                 second(r, g)
-        for g in range(groups):
-            base(0, g, next_bank())
-        z_banks = [banks[b] for b in free[:groups]]
-        for b in free[:groups]:
-            free.remove(b)
-        for g in range(groups):
-            base(1, g, z_banks[g])
-
-        place_s(0, qs[0])
-        place_s(1, qs[1])
-        finish_turned(0, 0)
-        for r in range(1, ROW_TILES - 1):
-            finish_gpsimd(r)
-            place_q(qs[1], q_sb[r + 1][:], 0, I)
-            place_s(r + 1, qs[1])
+            nc.gpsimd.tensor_tensor(s_sb[r][:], p_sb[r][:], qs[r][:], ADD)
+        for r in range(last):
             for g in range(groups):
-                base(r + 1, g, z_banks[g])
-            finish_turned(r, GP_COLS)
-        for g in range(groups):
-            finish_vector(ROW_TILES - 1, g, z_banks[g])
+                base(r, g, z_sb[r][:, BANK * g : BANK * (g + 1)])
+        base(last, groups - 1, z_end[:])
+        z_banks = [base(last, g, None) for g in range(groups - 1)]
+
+        for r in range(last):
+            place_s(r)
+            for lo in range(0, T, HALF):
+                nc.gpsimd.tensor_tensor(y_sb[r][:, lo : lo + HALF], z_sb[r][:, lo : lo + HALF], sp[r % 2][:, lo : lo + HALF], ADD)
+                store(r, lo, lo + HALF, y_sb[r])
+        place_s(last)
+        y_last = z_sb[last - 1]
+        for lo, hi in TAIL:
+            nc.vector.tensor_tensor(y_last[:, lo:hi], z_banks[lo // BANK][:, lo % BANK : lo % BANK + hi - lo], sp[last % 2][:, lo:hi], ADD)
+            store(last, lo, hi, y_last)
+        nc.gpsimd.tensor_tensor(y_last[:, T - BANK : T], z_end[:], sp[last % 2][:, T - BANK : T], ADD)
+        store(last, T - BANK, T, y_last)

from contextlib import ExitStack

import concourse.mybir as mybir

K, T, J, I, N = 512, 2048, 1024, 512, 512
FLOPS = 2 * K * N * (T + J + I)

F32 = mybir.dt.float32
BF16 = mybir.dt.bfloat16
I32 = mybir.dt.int32
U32 = mybir.dt.uint32
U16 = mybir.dt.uint16
U8 = mybir.dt.uint8
FP8X4 = mybir.dt.float8_e4m3fn_x4
FP4X4 = mybir.dt.float4_e2m1fn_x4
ADD = mybir.AluOpType.add

P = 128
PACK = 4
BANK = 512
BANKS = 8
ROW_TILES = N // P
CHUNKS = ((0, 128), (128, 256), (256, 512))
FILL = 512
HALF = T // 2
TAIL = ((0, 256), (256, 512), (512, 1024), (1024, 1536))


def tile_list_three_tiers_nested_kernel(tc, xq_words, xq_scales, wa_words, wa_scales, xb_words, xb_scales, wb_words, wb_scales, xc, wc_words, wc_scales, offs, offs2, out):
    nc = tc.nc
    with ExitStack() as ctx:
        keep = ctx.enter_context(tc.tile_pool(name="keep", bufs=1))
        psum = ctx.enter_context(tc.psum_pool(name="psum", bufs=1))

        idx = keep.tile([P, J // 16], U16, name="idx")
        idx2 = keep.tile([P, I // 16], U16, name="idx2")

        def held(name, shape, dtype, tag=None):
            return keep.tile(shape, dtype, name=name, tag=tag or name, align_bytes=64)

        wa = held("wa", [P, N], U32)
        wb = held("wb", [P, N], U32)
        wc = [held("wc%d" % h, [P, N // 2], U32) for h in range(2)]
        xq = held("xq", [P, 2 * T], U8)
        xb = held("xb", [P, 2 * J], U8)
        wc_s = held("wc_s", [P, N], U8)
        second_s = held("second_s", [P, N + J], U8)
        base_s = held("base_s", [P, N + T], U8)
        wb_s, xb_s = second_s[:, 0:N], second_s[:, N : N + J]
        wa_s, xq_s = base_s[:, 0:N], base_s[:, N : N + T]
        xc_raw = [held("xc_raw%d" % c, [P, PACK, hi - lo], F32) for c, (lo, hi) in enumerate(CHUNKS)]
        xc_bf = [held("xc_bf%d" % c, [P, hi - lo, PACK], BF16) for c, (lo, hi) in enumerate(CHUNKS)]
        xcq = held("xcq", [P, I], U32)
        xcq_s = held("xcq_s", [P, I], U8)
        q_sb = [held("q_sb%d" % r, [P, I], F32) for r in range(ROW_TILES)]
        p_sb = [held("p_sb%d" % r, [P, J], F32) for r in range(ROW_TILES)]
        s_sb = [held("s_sb%d" % r, [P, J], F32) for r in range(ROW_TILES)]
        z_sb = [held("z_sb%d" % r, [P, T], F32) for r in range(ROW_TILES - 1)]
        y_sb = [held("y_sb%d" % r, [P, T], F32) for r in range(ROW_TILES - 1)]
        z_end = held("z_end", [P, BANK], F32)
        qs = [held("qs%d" % b, [P, J], F32) for b in range(2)]
        banks = [psum.tile([P, BANK], F32, name="bank%d" % b) for b in range(BANKS)]
        free = list(range(BANKS))

        def next_bank():
            b = free[0]
            free.remove(b)
            free.append(b)
            return banks[b]

        def load_words(dst, src):
            nc.sync.dma_start(out=dst[:].bitcast(I32), in_=src.bitcast(I32))

        def load_fp8(dst, words):
            load_words(dst, words[0].rearrange("p n t -> p (n t)"))

        def load_scales(dst, scales):
            for quad in range(4):
                nc.sync.dma_start(out=dst[32 * quad : 32 * quad + 4, :].bitcast(I32), in_=scales[0, 4 * quad : 4 * quad + 4, :].bitcast(I32))

        def load_xc(c):
            lo, hi = CHUNKS[c]
            nc.sync.dma_start(out=xc_raw[c][:], in_=xc[:, lo:hi].rearrange("(p t) w -> p t w", t=PACK))

        nc.vector.memset(wc_s[:].bitcast(I32), 0)
        nc.vector.memset(second_s[:].bitcast(I32), 0)
        nc.vector.memset(base_s[:].bitcast(I32), 0)

        load_xc(0)
        load_scales(wc_s[:], wc_scales)
        wc_rows = wc_words[0].rearrange("p n t -> p (n t)")
        load_words(wc[0], wc_rows[:, 0 : 2 * N])
        nc.sync.dma_start(idx2[:], offs2)
        load_xc(1)
        load_xc(2)
        load_words(wc[1], wc_rows[:, 2 * N : 4 * N])
        load_fp8(wb, wb_words)
        load_words(xb, xb_words[0])
        load_scales(wb_s, wb_scales)
        load_scales(xb_s, xb_scales)
        nc.sync.dma_start(idx[:], offs)
        load_fp8(wa, wa_words)
        load_words(xq, xq_words[0])
        load_scales(wa_s, wa_scales)
        load_scales(xq_s, xq_scales)

        def weave(c, copy):
            copy(out=xc_bf[c][:].rearrange("p (g i) t -> p g t i", i=4), in_=xc_raw[c][:].rearrange("p t (g i) -> p g t i", i=4))

        def quantize(c):
            lo, hi = CHUNKS[c]
            nc.vector.quantize_mx(out=xcq[:, lo:hi].bitcast(FP8X4), scales=xcq_s[:, lo:hi], in_=xc_bf[c][:].rearrange("p w t -> p (w t)"))

        def product(bank, w, w_s, r, x, x_s):
            nc.tensor.matmul_mx(out=bank, lhsT=w.bitcast(FP8X4), lhsT_scale=w_s[:, r * P : (r + 1) * P], rhs=x, rhs_scale=x_s, start=True, stop=True)

        def third(r, lo, hi, dst):
            bank = next_bank()[:, 0 : hi - lo]
            product(bank, wc[r // 2][:, r % 2 * P : (r % 2 + 1) * P], wc_s, r, xcq[:, lo:hi].bitcast(FP8X4), xcq_s[:, lo:hi])
            nc.scalar.copy(out=dst, in_=bank)

        def fp4_product(bank, w, w_s, r, x, x_s, g):
            product(bank[:], w[:, r * P : (r + 1) * P], w_s, r, x[:, 2 * BANK * g : 2 * BANK * (g + 1)].bitcast(FP4X4), x_s[:, BANK * g : BANK * (g + 1)])

        def second(r, g):
            bank = next_bank()
            fp4_product(bank, wb, wb_s, r, xb, xb_s, g)
            nc.scalar.copy(out=p_sb[r][:, BANK * g : BANK * (g + 1)], in_=bank[:])

        def base(r, g, dst):
            bank = next_bank()
            fp4_product(bank, wa, wa_s, r, xq, xq_s, g)
            if dst is not None:
                nc.scalar.copy(out=dst, in_=bank[:])
            return bank

        def place_q(window, src, lo, hi):
            nc.vector.tensor_copy(window[:].indirect(idx2[:, lo // 16 : hi // 16]), src)

        def place_s(r):
            nc.vector.tensor_copy(sp[r % 2][:].indirect(idx[:]), s_sb[r][:])

        def store(r, lo, hi, src):
            nc.sync.dma_start(out=out[r * P : (r + 1) * P, lo:hi], in_=src[:, lo:hi])

        def clear(window):
            for lo in range(0, window.shape[1], FILL):
                nc.vector.memset(window[:, lo : lo + FILL], 0.0)

        weave(0, nc.vector.tensor_copy)
        quantize(0)
        weave(1, nc.scalar.copy)
        quantize(1)
        clear(qs[0])
        clear(qs[1])
        for c in range(2):
            lo, hi = CHUNKS[c]
            if c == 1:
                weave(2, nc.scalar.copy)
                quantize(2)
            for r in range(2):
                dst = xc_raw[2][:, 0, 0 : hi - lo] if (c, r) == (1, 1) else q_sb[r][:, lo:hi]
                third(r, lo, hi, dst)
                place_q(qs[r], dst, lo, hi)
        lo, hi = CHUNKS[2]
        for r in range(2):
            third(r, lo, hi, q_sb[r][:, lo:hi])
            place_q(qs[r], q_sb[r][:, lo:hi], lo, hi)
        for r in range(2, ROW_TILES):
            third(r, 0, I, q_sb[r][:])
        for r, tag in ((2, "xc_bf2"), (3, "xc_raw2")):
            qs.append(held("qs%d" % r, [P, J], F32, tag))
            nc.gpsimd.memset(qs[r][:], 0.0)
            place_q(qs[r], q_sb[r][:], 0, I)
        sp = [held("sp0", [P, T], F32, "wc1"), held("sp1", [P, T], F32, "xcq")]
        for window in sp:
            nc.gpsimd.memset(window[:], 0.0)

        groups = T // BANK
        last = ROW_TILES - 1
        for r in range(ROW_TILES):
            for g in range(J // BANK):
                second(r, g)
            nc.gpsimd.tensor_tensor(s_sb[r][:], p_sb[r][:], qs[r][:], ADD)
        for r in range(last):
            for g in range(groups):
                base(r, g, z_sb[r][:, BANK * g : BANK * (g + 1)])
        base(last, groups - 1, z_end[:])
        z_banks = [base(last, g, None) for g in range(groups - 1)]

        for r in range(last):
            place_s(r)
            for lo in range(0, T, HALF):
                nc.gpsimd.tensor_tensor(y_sb[r][:, lo : lo + HALF], z_sb[r][:, lo : lo + HALF], sp[r % 2][:, lo : lo + HALF], ADD)
                store(r, lo, lo + HALF, y_sb[r])
        place_s(last)
        y_last = z_sb[last - 1]
        for lo, hi in TAIL:
            nc.vector.tensor_tensor(y_last[:, lo:hi], z_banks[lo // BANK][:, lo % BANK : lo % BANK + hi - lo], sp[last % 2][:, lo:hi], ADD)
            store(last, lo, hi, y_last)
        nc.gpsimd.tensor_tensor(y_last[:, T - BANK : T], z_end[:], sp[last % 2][:, T - BANK : T], ADD)
        store(last, T - BANK, T, y_last)
